import numpy as np
import ml_dtypes


def mxq(x, axis, fmt="e4m3"):
    dtype, down = {"e4m3": (ml_dtypes.float8_e4m3fn, 7), "e5m2": (ml_dtypes.float8_e5m2, 14)}[fmt]
    v = np.moveaxis(np.asarray(x, np.float32).astype(ml_dtypes.bfloat16).astype(np.float64), axis, -1)
    blocks = v.reshape(v.shape[:-1] + (-1, 32))
    amax = np.abs(blocks).max(-1, keepdims=True)
    byte = np.maximum(np.where(amax > 0, np.frexp(amax)[1] - 1 + 127, 0) - down, 1)
    scale = np.exp2(byte - 127.0)
    codes = (blocks / scale).astype(np.float32).astype(dtype).astype(np.float64)
    return np.moveaxis((codes * scale).reshape(v.shape), -1, axis)


WIDE = False


def mx_kscale(k):
    if not WIDE:
        return np.ones(k)
    levels = np.array([10, -10, 5, -5, 0])
    if k % 512:
        return np.exp2(np.random.permutation(np.resize(levels, k // 32))).repeat(32)
    a = np.empty((k // 512, 16))
    for p in range(k // 512):
        a[p, :8] = np.random.permutation(np.resize(levels, 8))
        for g in range(8):
            far = levels[np.abs(levels - a[p, g]) >= 10]
            a[p, g + 8] = far[np.random.randint(len(far))]
    return np.exp2(a.ravel()).repeat(32)


def f64(x):
    return np.asarray(x).astype(np.float64)


def striped(idx):
    return np.tile(idx.reshape(-1, 16).T, (8, 1)).astype(np.uint16)


def unstriped(offs):
    return offs[:16].T.reshape(-1).astype(np.int64)


def striped8(idx):
    return np.concatenate([x.reshape(-1, 16).T for x in idx]).astype(np.uint16)


def runs(offs, k):
    lists = np.stack([offs[16 * r : 16 * r + 16].T.reshape(-1) for r in range(8)]).astype(np.int64)
    return lists[np.arange(k) % 512 // 64]


def pack_weight(w):
    k, n = w.shape
    w = f64(np.asarray(w, np.float32).astype(ml_dtypes.bfloat16)).reshape(k // 32, 32, n)
    amax = np.abs(w).max(1)
    byte = np.clip(np.where(amax > 0, np.frexp(amax)[1] - 1 + 127 - 7, 1), 1, 254)
    scaled = (w * np.exp2(127.0 - byte)[:, None, :]).reshape(k, n).astype(np.float32)
    words = np.ascontiguousarray(scaled.reshape(k // 512, 128, 4, n).transpose(0, 1, 3, 2)).astype(ml_dtypes.float8_e4m3fn).view(np.uint8)
    return words, np.ascontiguousarray(byte.astype(np.uint8).reshape(k // 512, 16, n))


def unpack_weight(words, scales):
    g, p, n, _ = words.shape
    vals = np.ascontiguousarray(words).view(ml_dtypes.float8_e4m3fn).astype(np.float64) * np.repeat(np.exp2(scales.astype(np.float64) - 127.0), 8, axis=1)[..., None]
    return vals.transpose(0, 1, 3, 2).reshape(g * 512, n)


K, T, S, N, H, W, G, U = 512, 2048, 256, 512, 512, 192, 2048, 128


def setup_inputs():
    n = np.random.standard_normal
    s = mx_kscale(K)[:, None]
    u = mx_kscale(K)
    packed_xT = pack_weight(n((K, T)) * s)
    packed_dT = pack_weight(n((K, G)) / s)
    return {
        "x_words": packed_xT[0],
        "x_scales": packed_xT[1],
        "w1": (n((K, H)) / np.sqrt(K) / s).astype(np.float32),
        "gn": (np.random.uniform(0.5, 1.5, (H, 1)) * u[:, None]).astype(np.float32),
        "w2": (n((H, N)) / np.sqrt(H) / u[:, None]).astype(np.float32),
        "d_words": packed_dT[0],
        "d_scales": packed_dT[1],
        "offs": striped(np.random.permutation(T)[:S]),
        "n1": striped(np.random.permutation(S)[:W]),
        "n2": striped(np.random.permutation(S)[:W]),
        "two": striped(np.random.permutation(T)[:S]),
        "k1": striped8(np.random.randint(0, G, (8, H))),
        "n3": striped(np.random.permutation(S)[:U]),
        "n4": striped(np.random.permutation(S)[:U]),
    }


def reference(x_words, x_scales, w1, gn, w2, d_words, d_scales, offs, n1, n2, two, k1, n3, n4):
    d_k1 = unpack_weight(d_words, d_scales)[np.arange(K)[:, None], runs(k1, K)]
    x_two = unpack_weight(x_words, x_scales)[:, unstriped(two)]
    b = 0.0625 * (d_k1.T @ x_two)
    xq = unpack_weight(x_words, x_scales)[:, unstriped(offs)]
    y = mxq(f64(w1), 0, "e4m3").T @ xq
    old = y[:, unstriped(n1)]
    pa = y[:, unstriped(n2)]
    ra = old - (0.5 * pa)
    ds = y.copy()
    ds[:, unstriped(n1)] = ra
    z = f64(gn) * ds
    a = mxq(f64(w2), 0, "e4m3").T @ mxq(z, 0, "e4m3")
    ra2 = b[:, unstriped(n4)] - (0.5 * a[:, unstriped(n3)])
    out = a.copy()
    out[:, unstriped(n3)] = ra2
    return out

@@ -1,0 +1,208 @@
+from contextlib import ExitStack
+
+import concourse.mybir as mybir
+
+K, T, S, N, H, W, G, U = 512, 2048, 256, 512, 512, 192, 2048, 128
+FLOPS = 3 * 2 * 512 * 512 * 256
+
+F32 = mybir.dt.float32
+BF16 = mybir.dt.bfloat16
+I32 = mybir.dt.int32
+U32 = mybir.dt.uint32
+U16 = mybir.dt.uint16
+U8 = mybir.dt.uint8
+FP8X4 = mybir.dt.float8_e4m3fn_x4
+COPY = mybir.ActivationFunctionType.Copy
+MULT = mybir.AluOpType.mult
+ADD = mybir.AluOpType.add
+
+P = 128
+PACK = 4
+TILES = 4
+
+
+def tile_picked_cdjoinputbkdif_none_p_kernel(
+    tc, x_words, x_scales, w1, gn, w2, d_words, d_scales, offs, n1, n2, two, k1, n3, n4, out
+):
+    nc = tc.nc
+    with ExitStack() as ctx:
+        lists = ctx.enter_context(tc.tile_pool(name="lists", bufs=1))
+        sb = ctx.enter_context(tc.tile_pool(name="sb", bufs=1))
+        psum = ctx.enter_context(tc.psum_pool(name="psum", bufs=1))
+
+        def load_list(src, name):
+            t = lists.tile([P, src.shape[1]], U16, name=name)
+            nc.sync.dma_start(t[:], src)
+            return t
+
+        def load_words(src, name, tag):
+            t = sb.tile([P, src.shape[2]], I32, name=name, tag=tag, align_bytes=64)
+            nc.sync.dma_start(t[:], src[0].rearrange("p c r -> p (c r)").bitcast(I32))
+            return t
+
+        xs_win = sb.tile([P, T], U8, name="xs_win", align_bytes=64)
+        ds_win = sb.tile([P, G], U8, name="ds_win", align_bytes=64)
+        d_plane = sb.tile([P, H], U8, name="d_plane", align_bytes=64)
+        nc.vector.memset(xs_win[:].bitcast(I32), 0)
+        nc.vector.memset(ds_win[:].bitcast(I32), 0)
+        nc.vector.memset(d_plane[:].bitcast(I32), 0)
+
+        half = H // 2
+        w1_rows = w1.rearrange("(p j) c -> p j c", j=PACK)
+        w1_raw = [
+            sb.tile([P, PACK, half], F32, name="w1_raw%d" % h, tag="stage%d" % h, align_bytes=64) for h in range(2)
+        ]
+        offs_t = load_list(offs, "offs_t")
+        nc.sync.dma_start(w1_raw[0][:], w1_rows[:, :, 0:half])
+        k1_t = load_list(k1, "k1_t")
+        two_t = load_list(two, "two_t")
+        n1_t = load_list(n1, "n1_t")
+        n2_t = load_list(n2, "n2_t")
+        n4_t = load_list(n4, "n4_t")
+        nc.sync.dma_start(w1_raw[1][:], w1_rows[:, :, half:H])
+        x_win = load_words(x_words, "x_win", "x_win")
+        n3_t = load_list(n3, "n3_t")
+        for q in range(4):
+            nc.scalar.dma_start(
+                xs_win[32 * q : 32 * q + 4, :].bitcast(I32), x_scales[0, 4 * q : 4 * q + 4, :].bitcast(I32)
+            )
+        nc.scalar.dma_start(ds_win[0:P:8, :].bitcast(I32), d_scales[0].bitcast(I32))
+        gn_t = sb.tile([P, PACK], F32, name="gn_t")
+        nc.gpsimd.dma_start(gn_t[:], gn.rearrange("(p t) one -> p (t one)", t=PACK))
+
+        w1_bf = sb.tile([P, TILES, P, PACK], BF16, name="w1_bf", align_bytes=64)
+
+        def cast_w1(copy, h, m0, m1):
+            src = w1_raw[h][:, :, 4 * m0 : 4 * m1].rearrange("p j (m t) -> p m j t", t=TILES)
+            dst = w1_bf[:, :, h * (P // 2) + m0 : h * (P // 2) + m1, :].rearrange("p t m j -> p m j t")
+            copy(dst, src)
+
+        cast_w1(nc.scalar.copy, 0, 0, 32)
+        cast_w1(nc.vector.tensor_copy, 0, 32, 64)
+        cast_w1(nc.vector.tensor_copy, 1, 0, 64)
+        d_win = load_words(d_words, "d_win", "stage1")
+        w2_raw = sb.tile([P, PACK, N], F32, name="w2_raw", tag="stage0", align_bytes=64)
+        nc.sync.dma_start(w2_raw[:], w2.rearrange("(p j) c -> p j c", j=PACK))
+        w1_codes = sb.tile([P, H], U32, name="w1_codes", align_bytes=64)
+        w1_plane = sb.tile([P, H], U8, name="w1_plane", align_bytes=64)
+        nc.vector.quantize_mx(
+            out=w1_codes[:].bitcast(FP8X4), scales=w1_plane[:], in_=w1_bf[:].rearrange("p t m j -> p (t m j)")
+        )
+
+        xq_plane = sb.tile([P, S], U8, name="xq_plane", align_bytes=64)
+        nc.vector.tensor_copy(xq_plane[:], xs_win[:].indirect(offs_t[:]))
+        xq_codes = sb.tile([P, S], U32, name="xq_codes", align_bytes=64)
+        nc.vector.tensor_copy(xq_codes[:], x_win[:].bitcast(U32).indirect(offs_t[:]))
+
+        ds = []
+        for t in range(TILES):
+            acc = psum.tile([P, S], F32, name="acc%d" % t)
+            cols = slice(t * P, (t + 1) * P)
+            nc.tensor.matmul_mx(
+                out=acc[:], lhsT=w1_codes[:, cols].bitcast(FP8X4), lhsT_scale=w1_plane[:, cols],
+                rhs=xq_codes[:].bitcast(FP8X4), rhs_scale=xq_plane[:], start=True, stop=True,
+            )
+            y = sb.tile([P, S], F32, name="y%d" % t)
+            if t == 0:
+                nc.scalar.copy(y[:], acc[:])
+            else:
+                nc.vector.tensor_copy(y[:], acc[:])
+            ds.append(y)
+
+        d_bytes = sb.tile([P, H], U8, name="d_bytes", align_bytes=64)
+        nc.vector.tensor_copy(d_bytes[:], ds_win[:].indirect(k1_t[:]))
+        for a in range(4):
+            nc.gpsimd.dma_start(d_plane[a:P:32, :].bitcast(I32), d_bytes[8 * a : P : 32, :].bitcast(I32))
+        xt_plane = sb.tile([P, S], U8, name="xt_plane", align_bytes=64)
+        nc.vector.tensor_copy(xt_plane[:], xs_win[:].indirect(two_t[:]))
+        xt_codes = sb.tile([P, S], U32, name="xt_codes", align_bytes=64)
+        nc.vector.tensor_copy(xt_codes[:], x_win[:].bitcast(U32).indirect(two_t[:]))
+        d_codes = sb.tile([P, H], U32, name="d_codes", align_bytes=64)
+        for h in range(2):
+            nc.vector.tensor_copy(
+                d_codes[:, h * half : (h + 1) * half],
+                d_win[:].bitcast(U32).indirect(k1_t[:, h * half // 16 : (h + 1) * half // 16]),
+            )
+
+        ra = []
+        for pair in range(2):
+            old = sb.tile([P, 2, W], F32, name="old%d" % pair)
+            pa = sb.tile([P, 2, W], F32, name="pa%d" % pair)
+            for e in range(2):
+                y = ds[2 * pair + e]
+                nc.scalar.activation(old[:, e, :], y[:].indirect(n1_t[:]), COPY)
+                nc.scalar.activation(pa[:, e, :], y[:].indirect(n2_t[:]), COPY)
+            r = sb.tile([P, 2, W], F32, name="ra%d" % pair, tag=("ra0", "stage1")[pair], align_bytes=64)
+            nc.vector.scalar_tensor_tensor(
+                r[:].rearrange("p e w -> p (e w)"), pa[:].rearrange("p e w -> p (e w)"), -0.5,
+                old[:].rearrange("p e w -> p (e w)"), MULT, ADD,
+            )
+            ra.append(r)
+
+        w2_bf = sb.tile([P, N, PACK], BF16, name="w2_bf", align_bytes=64)
+        for h in range(2):
+            cols = slice(h * half, (h + 1) * half)
+            nc.vector.tensor_copy(
+                w2_bf[:, cols, :].rearrange("p (c i) j -> p c j i", i=4),
+                w2_raw[:, :, cols].rearrange("p j (c i) -> p c j i", i=4),
+            )
+        w2_codes = sb.tile([P, N], U32, name="w2_codes", align_bytes=64)
+        w2_plane = sb.tile([P, N], U8, name="w2_plane", align_bytes=64)
+        nc.vector.quantize_mx(
+            out=w2_codes[:].bitcast(FP8X4), scales=w2_plane[:], in_=w2_bf[:].rearrange("p c j -> p (c j)")
+        )
+
+        z_bf = sb.tile([P, S, PACK], BF16, name="z_bf", tag="w2_bf", align_bytes=64)
+        for t in range(TILES):
+            nc.scalar.activation(ds[t][:].indirect(n1_t[:]), ra[t // 2][:, t % 2, :], COPY)
+            nc.vector.tensor_scalar(z_bf[:, :, t], ds[t][:], gn_t[:, t : t + 1], None, MULT)
+
+        bg = []
+        for pair in range(2):
+            acc = psum.tile([P, 2, S], F32, name="bacc%d" % pair)
+            for e in range(2):
+                cols = slice((2 * pair + e) * P, (2 * pair + e + 1) * P)
+                nc.tensor.matmul_mx(
+                    out=acc[:, e, :], lhsT=d_codes[:, cols].bitcast(FP8X4), lhsT_scale=d_plane[:, cols],
+                    rhs=xt_codes[:].bitcast(FP8X4), rhs_scale=xt_plane[:], start=True, stop=True,
+                )
+            b = sb.tile([P, 2, S], F32, name="b%d" % pair, tag=("b0", "stage1")[pair], align_bytes=64)
+            if pair == 0:
+                nc.vector.tensor_scalar(b[:], acc[:], 0.0625, None, MULT)
+            else:
+                nc.scalar.activation(b[:], acc[:], COPY, scale=0.0625)
+            g = sb.tile([P, 2, U], F32, name="bg%d" % pair, tag=("ra0", "bg1")[pair], align_bytes=64)
+            for e in range(2):
+                nc.scalar.activation(g[:, e, :], b[:, e, :].indirect(n4_t[:]), COPY)
+            bg.append(g)
+
+        z_codes = sb.tile([P, S], U32, name="z_codes", align_bytes=64)
+        z_plane = sb.tile([P, S], U8, name="z_plane", align_bytes=64)
+        nc.vector.quantize_mx(
+            out=z_codes[:].bitcast(FP8X4), scales=z_plane[:], in_=z_bf[:].rearrange("p c j -> p (c j)")
+        )
+
+        res = []
+        ra2 = []
+        for t in range(TILES):
+            acc = psum.tile([P, S], F32, name="acc%d" % t)
+            cols = slice(t * P, (t + 1) * P)
+            nc.tensor.matmul_mx(
+                out=acc[:], lhsT=w2_codes[:, cols].bitcast(FP8X4), lhsT_scale=w2_plane[:, cols],
+                rhs=z_codes[:].bitcast(FP8X4), rhs_scale=z_plane[:], start=True, stop=True,
+            )
+            a_t = sb.tile([P, S], F32, name="a%d" % t)
+            if t == 0:
+                nc.scalar.copy(a_t[:], acc[:])
+            else:
+                nc.vector.tensor_copy(a_t[:], acc[:])
+            res.append(a_t)
+        for t in range(TILES):
+            ag = sb.tile([P, U], F32, name="ag%d" % t)
+            nc.scalar.activation(ag[:], res[t][:].indirect(n3_t[:]), COPY)
+            r2 = sb.tile([P, U], F32, name="ra2_%d" % t)
+            nc.vector.scalar_tensor_tensor(r2[:], ag[:], -0.5, bg[t // 2][:, t % 2, :], MULT, ADD)
+            ra2.append(r2)
+        for t in range(TILES):
+            nc.scalar.activation(res[t][:].indirect(n3_t[:]), ra2[t][:], COPY)
+            nc.sync.dma_start(out[t * P : (t + 1) * P, :], res[t][:])

@@ -50,25 +50,28 @@ def tile_picked_cdjoinputbkdif_none_p_kernel(
         half = H // 2
         w1_rows = w1.rearrange("(p j) c -> p j c", j=PACK)
         w1_raw = [
-            sb.tile([P, PACK, half], F32, name="w1_raw%d" % h, tag="stage%d" % h, align_bytes=64) for h in range(2)
+            sb.tile([P, PACK, half], F32, name="w1_raw%d" % h) for h in range(2)
         ]
-        offs_t = load_list(offs, "offs_t")
         nc.sync.dma_start(w1_raw[0][:], w1_rows[:, :, 0:half])
-        k1_t = load_list(k1, "k1_t")
-        two_t = load_list(two, "two_t")
-        n1_t = load_list(n1, "n1_t")
-        n2_t = load_list(n2, "n2_t")
-        n4_t = load_list(n4, "n4_t")
-        nc.sync.dma_start(w1_raw[1][:], w1_rows[:, :, half:H])
-        x_win = load_words(x_words, "x_win", "x_win")
-        n3_t = load_list(n3, "n3_t")
         for q in range(4):
-            nc.scalar.dma_start(
+            nc.sync.dma_start(
                 xs_win[32 * q : 32 * q + 4, :].bitcast(I32), x_scales[0, 4 * q : 4 * q + 4, :].bitcast(I32)
             )
-        nc.scalar.dma_start(ds_win[0:P:8, :].bitcast(I32), d_scales[0].bitcast(I32))
+        offs_t = load_list(offs, "offs_t")
+        nc.sync.dma_start(w1_raw[1][:], w1_rows[:, :, half:H])
+        x_win = load_words(x_words, "x_win", "x_win")
+        two_t = load_list(two, "two_t")
+        k1_t = load_list(k1, "k1_t")
+        nc.sync.dma_start(ds_win[0:P:8, :].bitcast(I32), d_scales[0].bitcast(I32))
+        n1_t = load_list(n1, "n1_t")
+        n2_t = load_list(n2, "n2_t")
+        d_win = load_words(d_words, "d_win", "d_win")
+        w2_raw = sb.tile([P, PACK, N], F32, name="w2_raw", align_bytes=64)
+        nc.sync.dma_start(w2_raw[:], w2.rearrange("(p j) c -> p j c", j=PACK))
         gn_t = sb.tile([P, PACK], F32, name="gn_t")
-        nc.gpsimd.dma_start(gn_t[:], gn.rearrange("(p t) one -> p (t one)", t=PACK))
+        nc.sync.dma_start(gn_t[:], gn.rearrange("(p t) one -> p (t one)", t=PACK))
+        n4_t = load_list(n4, "n4_t")
+        n3_t = load_list(n3, "n3_t")
 
         w1_bf = sb.tile([P, TILES, P, PACK], BF16, name="w1_bf", align_bytes=64)
 
@@ -80,9 +83,6 @@ def tile_picked_cdjoinputbkdif_none_p_kernel(
         cast_w1(nc.scalar.copy, 0, 0, 32)
         cast_w1(nc.vector.tensor_copy, 0, 32, 64)
         cast_w1(nc.vector.tensor_copy, 1, 0, 64)
-        d_win = load_words(d_words, "d_win", "stage1")
-        w2_raw = sb.tile([P, PACK, N], F32, name="w2_raw", tag="stage0", align_bytes=64)
-        nc.sync.dma_start(w2_raw[:], w2.rearrange("(p j) c -> p j c", j=PACK))
         w1_codes = sb.tile([P, H], U32, name="w1_codes", align_bytes=64)
         w1_plane = sb.tile([P, H], U8, name="w1_plane", align_bytes=64)
         nc.vector.quantize_mx(
@@ -112,7 +112,7 @@ def tile_picked_cdjoinputbkdif_none_p_kernel(
         d_bytes = sb.tile([P, H], U8, name="d_bytes", align_bytes=64)
         nc.vector.tensor_copy(d_bytes[:], ds_win[:].indirect(k1_t[:]))
         for a in range(4):
-            nc.gpsimd.dma_start(d_plane[a:P:32, :].bitcast(I32), d_bytes[8 * a : P : 32, :].bitcast(I32))
+            nc.sync.dma_start(d_plane[a:P:32, :].bitcast(I32), d_bytes[8 * a : P : 32, :].bitcast(I32))
         xt_plane = sb.tile([P, S], U8, name="xt_plane", align_bytes=64)
         nc.vector.tensor_copy(xt_plane[:], xs_win[:].indirect(two_t[:]))
         xt_codes = sb.tile([P, S], U32, name="xt_codes", align_bytes=64)
@@ -132,7 +132,7 @@ def tile_picked_cdjoinputbkdif_none_p_kernel(
                 y = ds[2 * pair + e]
                 nc.scalar.activation(old[:, e, :], y[:].indirect(n1_t[:]), COPY)
                 nc.scalar.activation(pa[:, e, :], y[:].indirect(n2_t[:]), COPY)
-            r = sb.tile([P, 2, W], F32, name="ra%d" % pair, tag=("ra0", "stage1")[pair], align_bytes=64)
+            r = sb.tile([P, 2, W], F32, name="ra%d" % pair, tag=("ra0", "d_win")[pair], align_bytes=64)
             nc.vector.scalar_tensor_tensor(
                 r[:].rearrange("p e w -> p (e w)"), pa[:].rearrange("p e w -> p (e w)"), -0.5,
                 old[:].rearrange("p e w -> p (e w)"), MULT, ADD,
@@ -146,7 +146,19 @@ def tile_picked_cdjoinputbkdif_none_p_kernel(
                 w2_bf[:, cols, :].rearrange("p (c i) j -> p c j i", i=4),
                 w2_raw[:, :, cols].rearrange("p j (c i) -> p c j i", i=4),
             )
-        w2_codes = sb.tile([P, N], U32, name="w2_codes", align_bytes=64)
+        b_acc = []
+        for pair in range(2):
+            acc = psum.tile([P, 2, S], F32, name="bacc%d" % pair)
+            for e in range(2):
+                cols = slice((2 * pair + e) * P, (2 * pair + e + 1) * P)
+                nc.tensor.matmul_mx(
+                    out=acc[:, e, :], lhsT=d_codes[:, cols].bitcast(FP8X4), lhsT_scale=d_plane[:, cols],
+                    rhs=xt_codes[:].bitcast(FP8X4), rhs_scale=xt_plane[:], start=True, stop=True,
+                )
+            b_acc.append(acc)
+        b1 = sb.tile([P, 2, S], F32, name="b1")
+        nc.vector.tensor_scalar(b1[:], b_acc[1][:], 0.0625, None, MULT)
+        w2_codes = sb.tile([P, N], U32, name="w2_codes", tag="d_codes", align_bytes=64)
         w2_plane = sb.tile([P, N], U8, name="w2_plane", align_bytes=64)
         nc.vector.quantize_mx(
             out=w2_codes[:].bitcast(FP8X4), scales=w2_plane[:], in_=w2_bf[:].rearrange("p c j -> p (c j)")
@@ -157,24 +169,14 @@ def tile_picked_cdjoinputbkdif_none_p_kernel(
             nc.scalar.activation(ds[t][:].indirect(n1_t[:]), ra[t // 2][:, t % 2, :], COPY)
             nc.vector.tensor_scalar(z_bf[:, :, t], ds[t][:], gn_t[:, t : t + 1], None, MULT)
 
+        b0 = sb.tile([P, 2, S], F32, name="b0", tag="d_win", align_bytes=64)
+        nc.scalar.activation(b0[:], b_acc[0][:], COPY, scale=0.0625)
         bg = []
-        for pair in range(2):
-            acc = psum.tile([P, 2, S], F32, name="bacc%d" % pair)
-            for e in range(2):
-                cols = slice((2 * pair + e) * P, (2 * pair + e + 1) * P)
-                nc.tensor.matmul_mx(
-                    out=acc[:, e, :], lhsT=d_codes[:, cols].bitcast(FP8X4), lhsT_scale=d_plane[:, cols],
-                    rhs=xt_codes[:].bitcast(FP8X4), rhs_scale=xt_plane[:], start=True, stop=True,
-                )
-            b = sb.tile([P, 2, S], F32, name="b%d" % pair, tag=("b0", "stage1")[pair], align_bytes=64)
-            if pair == 0:
-                nc.vector.tensor_scalar(b[:], acc[:], 0.0625, None, MULT)
-            else:
-                nc.scalar.activation(b[:], acc[:], COPY, scale=0.0625)
-            g = sb.tile([P, 2, U], F32, name="bg%d" % pair, tag=("ra0", "bg1")[pair], align_bytes=64)
+        for pair, b in ((1, b1), (0, b0)):
+            g = sb.tile([P, 2, U], F32, name="bg%d" % pair, tag=("bg0", "ra0")[pair], align_bytes=64)
             for e in range(2):
                 nc.scalar.activation(g[:, e, :], b[:, e, :].indirect(n4_t[:]), COPY)
-            bg.append(g)
+            bg.insert(0, g)
 
         z_codes = sb.tile([P, S], U32, name="z_codes", align_bytes=64)
         z_plane = sb.tile([P, S], U8, name="z_plane", align_bytes=64)

@@ -48,17 +48,11 @@ def tile_picked_cdjoinputbkdif_none_p_kernel(
         nc.vector.memset(d_plane[:].bitcast(I32), 0)
 
         half = H // 2
-        w1_rows = w1.rearrange("(p j) c -> p j c", j=PACK)
-        w1_raw = [
-            sb.tile([P, PACK, half], F32, name="w1_raw%d" % h) for h in range(2)
-        ]
-        nc.sync.dma_start(w1_raw[0][:], w1_rows[:, :, 0:half])
-        for q in range(4):
-            nc.sync.dma_start(
-                xs_win[32 * q : 32 * q + 4, :].bitcast(I32), x_scales[0, 4 * q : 4 * q + 4, :].bitcast(I32)
-            )
+        w1_raw = sb.tile([P, PACK, H], F32, name="w1_raw")
+        nc.sync.dma_start(w1_raw[:], w1.rearrange("(p j) c -> p j c", j=PACK))
+        for a in range(4):
+            nc.sync.dma_start(xs_win[a:P:32, :].bitcast(I32), x_scales[0, a:16:4, :].bitcast(I32))
         offs_t = load_list(offs, "offs_t")
-        nc.sync.dma_start(w1_raw[1][:], w1_rows[:, :, half:H])
         x_win = load_words(x_words, "x_win", "x_win")
         two_t = load_list(two, "two_t")
         k1_t = load_list(k1, "k1_t")
@@ -75,14 +69,13 @@ def tile_picked_cdjoinputbkdif_none_p_kernel(
 
         w1_bf = sb.tile([P, TILES, P, PACK], BF16, name="w1_bf", align_bytes=64)
 
-        def cast_w1(copy, h, m0, m1):
-            src = w1_raw[h][:, :, 4 * m0 : 4 * m1].rearrange("p j (m t) -> p m j t", t=TILES)
-            dst = w1_bf[:, :, h * (P // 2) + m0 : h * (P // 2) + m1, :].rearrange("p t m j -> p m j t")
+        def cast_w1(copy, m0, m1):
+            src = w1_raw[:, :, 4 * m0 : 4 * m1].rearrange("p j (m t) -> p m j t", t=TILES)
+            dst = w1_bf[:, :, m0:m1, :].rearrange("p t m j -> p m j t")
             copy(dst, src)
 
-        cast_w1(nc.scalar.copy, 0, 0, 32)
-        cast_w1(nc.vector.tensor_copy, 0, 32, 64)
-        cast_w1(nc.vector.tensor_copy, 1, 0, 64)
+        cast_w1(nc.scalar.copy, 0, 40)
+        cast_w1(nc.vector.tensor_copy, 40, 128)
         w1_codes = sb.tile([P, H], U32, name="w1_codes", align_bytes=64)
         w1_plane = sb.tile([P, H], U8, name="w1_plane", align_bytes=64)
         nc.vector.quantize_mx(
@@ -110,7 +103,11 @@ def tile_picked_cdjoinputbkdif_none_p_kernel(
             ds.append(y)
 
         d_bytes = sb.tile([P, H], U8, name="d_bytes", align_bytes=64)
-        nc.vector.tensor_copy(d_bytes[:], ds_win[:].indirect(k1_t[:]))
+        for h in range(2):
+            nc.vector.tensor_copy(
+                d_bytes[:, h * half : (h + 1) * half],
+                ds_win[:].indirect(k1_t[:, h * half // 16 : (h + 1) * half // 16]),
+            )
         for a in range(4):
             nc.sync.dma_start(d_plane[a:P:32, :].bitcast(I32), d_bytes[8 * a : P : 32, :].bitcast(I32))
         xt_plane = sb.tile([P, S], U8, name="xt_plane", align_bytes=64)
@@ -124,20 +121,27 @@ def tile_picked_cdjoinputbkdif_none_p_kernel(
                 d_win[:].bitcast(U32).indirect(k1_t[:, h * half // 16 : (h + 1) * half // 16]),
             )
 
-        ra = []
+        picked = []
         for pair in range(2):
             old = sb.tile([P, 2, W], F32, name="old%d" % pair)
-            pa = sb.tile([P, 2, W], F32, name="pa%d" % pair)
+            pa = sb.tile([P, 2, W], F32, name="pa%d" % pair, align_bytes=64)
             for e in range(2):
                 y = ds[2 * pair + e]
                 nc.scalar.activation(old[:, e, :], y[:].indirect(n1_t[:]), COPY)
                 nc.scalar.activation(pa[:, e, :], y[:].indirect(n2_t[:]), COPY)
+            picked.append((old, pa))
+
+        def combine(pair):
+            old, pa = picked[pair]
             r = sb.tile([P, 2, W], F32, name="ra%d" % pair, tag=("ra0", "d_win")[pair], align_bytes=64)
             nc.vector.scalar_tensor_tensor(
                 r[:].rearrange("p e w -> p (e w)"), pa[:].rearrange("p e w -> p (e w)"), -0.5,
                 old[:].rearrange("p e w -> p (e w)"), MULT, ADD,
             )
-            ra.append(r)
+            return r
+
+        ra = [combine(0)]
+        ra.append(combine(1))
 
         w2_bf = sb.tile([P, N, PACK], BF16, name="w2_bf", align_bytes=64)
         for h in range(2):
@@ -156,8 +160,6 @@ def tile_picked_cdjoinputbkdif_none_p_kernel(
                     rhs=xt_codes[:].bitcast(FP8X4), rhs_scale=xt_plane[:], start=True, stop=True,
                 )
             b_acc.append(acc)
-        b1 = sb.tile([P, 2, S], F32, name="b1")
-        nc.vector.tensor_scalar(b1[:], b_acc[1][:], 0.0625, None, MULT)
         w2_codes = sb.tile([P, N], U32, name="w2_codes", tag="d_codes", align_bytes=64)
         w2_plane = sb.tile([P, N], U8, name="w2_plane", align_bytes=64)
         nc.vector.quantize_mx(
@@ -169,14 +171,12 @@ def tile_picked_cdjoinputbkdif_none_p_kernel(
             nc.scalar.activation(ds[t][:].indirect(n1_t[:]), ra[t // 2][:, t % 2, :], COPY)
             nc.vector.tensor_scalar(z_bf[:, :, t], ds[t][:], gn_t[:, t : t + 1], None, MULT)
 
-        b0 = sb.tile([P, 2, S], F32, name="b0", tag="d_win", align_bytes=64)
-        nc.scalar.activation(b0[:], b_acc[0][:], COPY, scale=0.0625)
-        bg = []
-        for pair, b in ((1, b1), (0, b0)):
-            g = sb.tile([P, 2, U], F32, name="bg%d" % pair, tag=("bg0", "ra0")[pair], align_bytes=64)
-            for e in range(2):
-                nc.scalar.activation(g[:, e, :], b[:, e, :].indirect(n4_t[:]), COPY)
-            bg.insert(0, g)
+        b = sb.tile([P, TILES, S], F32, name="b", tag="d_win", align_bytes=64)
+        bg = sb.tile([P, TILES, U], F32, name="bg")
+        for pair in range(2):
+            nc.scalar.activation(b[:, 2 * pair : 2 * pair + 2, :], b_acc[pair][:], COPY, scale=0.0625)
+        for t in range(TILES):
+            nc.scalar.activation(bg[:, t, :], b[:, t, :].indirect(n4_t[:]), COPY)
 
         z_codes = sb.tile([P, S], U32, name="z_codes", align_bytes=64)
         z_plane = sb.tile([P, S], U8, name="z_plane", align_bytes=64)
@@ -184,8 +184,7 @@ def tile_picked_cdjoinputbkdif_none_p_kernel(
             out=z_codes[:].bitcast(FP8X4), scales=z_plane[:], in_=z_bf[:].rearrange("p c j -> p (c j)")
         )
 
-        res = []
-        ra2 = []
+        a_acc = []
         for t in range(TILES):
             acc = psum.tile([P, S], F32, name="acc%d" % t)
             cols = slice(t * P, (t + 1) * P)
@@ -193,18 +192,32 @@ def tile_picked_cdjoinputbkdif_none_p_kernel(
                 out=acc[:], lhsT=w2_codes[:, cols].bitcast(FP8X4), lhsT_scale=w2_plane[:, cols],
                 rhs=z_codes[:].bitcast(FP8X4), rhs_scale=z_plane[:], start=True, stop=True,
             )
-            a_t = sb.tile([P, S], F32, name="a%d" % t)
-            if t == 0:
-                nc.scalar.copy(a_t[:], acc[:])
-            else:
-                nc.vector.tensor_copy(a_t[:], acc[:])
-            res.append(a_t)
-        for t in range(TILES):
-            ag = sb.tile([P, U], F32, name="ag%d" % t)
+            a_acc.append(acc)
+        res = []
+        ra2 = [sb.tile([P, U], F32, name="ra2_%d" % t) for t in range(TILES)]
+
+        def fetch(t):
+            ag = sb.tile([P, U], F32, name="ag%d" % t, tag="ag%d" % t)
             nc.scalar.activation(ag[:], res[t][:].indirect(n3_t[:]), COPY)
-            r2 = sb.tile([P, U], F32, name="ra2_%d" % t)
-            nc.vector.scalar_tensor_tensor(r2[:], ag[:], -0.5, bg[t // 2][:, t % 2, :], MULT, ADD)
-            ra2.append(r2)
-        for t in range(TILES):
+            nc.vector.scalar_tensor_tensor(ra2[t][:], ag[:], -0.5, bg[:, t, :], MULT, ADD)
+
+        def put(t):
             nc.scalar.activation(res[t][:].indirect(n3_t[:]), ra2[t][:], COPY)
             nc.sync.dma_start(out[t * P : (t + 1) * P, :], res[t][:])
+
+        def empty(t, copy):
+            tag = "ag%d" % (t - 2) if t == 2 else "a%d" % t
+            res.append(sb.tile([P, S], F32, name="a%d" % t, tag=tag))
+            copy(res[t][:], a_acc[t][:])
+
+        empty(0, nc.vector.tensor_copy)
+        empty(1, nc.vector.tensor_copy)
+        fetch(0)
+        fetch(1)
+        empty(2, nc.vector.tensor_copy)
+        empty(3, nc.vector.tensor_copy)
+        put(0)
+        fetch(2)
+        fetch(3)
+        for t in range(1, TILES):
+            put(t)

from contextlib import ExitStack

import concourse.mybir as mybir

K, T, S, N, H, W, G, U = 512, 2048, 256, 512, 512, 192, 2048, 128
FLOPS = 3 * 2 * 512 * 512 * 256

F32 = mybir.dt.float32
BF16 = mybir.dt.bfloat16
I32 = mybir.dt.int32
U32 = mybir.dt.uint32
U16 = mybir.dt.uint16
U8 = mybir.dt.uint8
FP8X4 = mybir.dt.float8_e4m3fn_x4
COPY = mybir.ActivationFunctionType.Copy
MULT = mybir.AluOpType.mult
ADD = mybir.AluOpType.add

P = 128
PACK = 4
TILES = 4


def tile_picked_cdjoinputbkdif_none_p_kernel(
    tc, x_words, x_scales, w1, gn, w2, d_words, d_scales, offs, n1, n2, two, k1, n3, n4, out
):
    nc = tc.nc
    with ExitStack() as ctx:
        lists = ctx.enter_context(tc.tile_pool(name="lists", bufs=1))
        sb = ctx.enter_context(tc.tile_pool(name="sb", bufs=1))
        psum = ctx.enter_context(tc.psum_pool(name="psum", bufs=1))

        def load_list(src, name):
            t = lists.tile([P, src.shape[1]], U16, name=name)
            nc.sync.dma_start(t[:], src)
            return t

        def load_words(src, name, tag):
            t = sb.tile([P, src.shape[2]], I32, name=name, tag=tag, align_bytes=64)
            nc.sync.dma_start(t[:], src[0].rearrange("p c r -> p (c r)").bitcast(I32))
            return t

        xs_win = sb.tile([P, T], U8, name="xs_win", align_bytes=64)
        ds_win = sb.tile([P, G], U8, name="ds_win", align_bytes=64)
        d_plane = sb.tile([P, H], U8, name="d_plane", align_bytes=64)
        nc.vector.memset(xs_win[:].bitcast(I32), 0)
        nc.vector.memset(ds_win[:].bitcast(I32), 0)
        nc.vector.memset(d_plane[:].bitcast(I32), 0)

        half = H // 2
        w1_raw = sb.tile([P, PACK, H], F32, name="w1_raw")
        nc.sync.dma_start(w1_raw[:], w1.rearrange("(p j) c -> p j c", j=PACK))
        for a in range(4):
            nc.sync.dma_start(xs_win[a:P:32, :].bitcast(I32), x_scales[0, a:16:4, :].bitcast(I32))
        offs_t = load_list(offs, "offs_t")
        x_win = load_words(x_words, "x_win", "x_win")
        two_t = load_list(two, "two_t")
        k1_t = load_list(k1, "k1_t")
        nc.sync.dma_start(ds_win[0:P:8, :].bitcast(I32), d_scales[0].bitcast(I32))
        n1_t = load_list(n1, "n1_t")
        n2_t = load_list(n2, "n2_t")
        d_win = load_words(d_words, "d_win", "d_win")
        w2_raw = sb.tile([P, PACK, N], F32, name="w2_raw", align_bytes=64)
        nc.sync.dma_start(w2_raw[:], w2.rearrange("(p j) c -> p j c", j=PACK))
        gn_t = sb.tile([P, PACK], F32, name="gn_t")
        nc.sync.dma_start(gn_t[:], gn.rearrange("(p t) one -> p (t one)", t=PACK))
        n4_t = load_list(n4, "n4_t")
        n3_t = load_list(n3, "n3_t")

        w1_bf = sb.tile([P, TILES, P, PACK], BF16, name="w1_bf", align_bytes=64)

        def cast_w1(copy, m0, m1):
            src = w1_raw[:, :, 4 * m0 : 4 * m1].rearrange("p j (m t) -> p m j t", t=TILES)
            dst = w1_bf[:, :, m0:m1, :].rearrange("p t m j -> p m j t")
            copy(dst, src)

        cast_w1(nc.scalar.copy, 0, 40)
        cast_w1(nc.vector.tensor_copy, 40, 128)
        w1_codes = sb.tile([P, H], U32, name="w1_codes", align_bytes=64)
        w1_plane = sb.tile([P, H], U8, name="w1_plane", align_bytes=64)
        nc.vector.quantize_mx(
            out=w1_codes[:].bitcast(FP8X4), scales=w1_plane[:], in_=w1_bf[:].rearrange("p t m j -> p (t m j)")
        )

        xq_plane = sb.tile([P, S], U8, name="xq_plane", align_bytes=64)
        nc.vector.tensor_copy(xq_plane[:], xs_win[:].indirect(offs_t[:]))
        xq_codes = sb.tile([P, S], U32, name="xq_codes", align_bytes=64)
        nc.vector.tensor_copy(xq_codes[:], x_win[:].bitcast(U32).indirect(offs_t[:]))

        ds = []
        for t in range(TILES):
            acc = psum.tile([P, S], F32, name="acc%d" % t)
            cols = slice(t * P, (t + 1) * P)
            nc.tensor.matmul_mx(
                out=acc[:], lhsT=w1_codes[:, cols].bitcast(FP8X4), lhsT_scale=w1_plane[:, cols],
                rhs=xq_codes[:].bitcast(FP8X4), rhs_scale=xq_plane[:], start=True, stop=True,
            )
            y = sb.tile([P, S], F32, name="y%d" % t)
            if t == 0:
                nc.scalar.copy(y[:], acc[:])
            else:
                nc.vector.tensor_copy(y[:], acc[:])
            ds.append(y)

        d_bytes = sb.tile([P, H], U8, name="d_bytes", align_bytes=64)
        for h in range(2):
            nc.vector.tensor_copy(
                d_bytes[:, h * half : (h + 1) * half],
                ds_win[:].indirect(k1_t[:, h * half // 16 : (h + 1) * half // 16]),
            )
        for a in range(4):
            nc.sync.dma_start(d_plane[a:P:32, :].bitcast(I32), d_bytes[8 * a : P : 32, :].bitcast(I32))
        xt_plane = sb.tile([P, S], U8, name="xt_plane", align_bytes=64)
        nc.vector.tensor_copy(xt_plane[:], xs_win[:].indirect(two_t[:]))
        xt_codes = sb.tile([P, S], U32, name="xt_codes", align_bytes=64)
        nc.vector.tensor_copy(xt_codes[:], x_win[:].bitcast(U32).indirect(two_t[:]))
        d_codes = sb.tile([P, H], U32, name="d_codes", align_bytes=64)
        for h in range(2):
            nc.vector.tensor_copy(
                d_codes[:, h * half : (h + 1) * half],
                d_win[:].bitcast(U32).indirect(k1_t[:, h * half // 16 : (h + 1) * half // 16]),
            )

        picked = []
        for pair in range(2):
            old = sb.tile([P, 2, W], F32, name="old%d" % pair)
            pa = sb.tile([P, 2, W], F32, name="pa%d" % pair, align_bytes=64)
            for e in range(2):
                y = ds[2 * pair + e]
                nc.scalar.activation(old[:, e, :], y[:].indirect(n1_t[:]), COPY)
                nc.scalar.activation(pa[:, e, :], y[:].indirect(n2_t[:]), COPY)
            picked.append((old, pa))

        def combine(pair):
            old, pa = picked[pair]
            r = sb.tile([P, 2, W], F32, name="ra%d" % pair, tag=("ra0", "d_win")[pair], align_bytes=64)
            nc.vector.scalar_tensor_tensor(
                r[:].rearrange("p e w -> p (e w)"), pa[:].rearrange("p e w -> p (e w)"), -0.5,
                old[:].rearrange("p e w -> p (e w)"), MULT, ADD,
            )
            return r

        ra = [combine(0)]
        ra.append(combine(1))

        w2_bf = sb.tile([P, N, PACK], BF16, name="w2_bf", align_bytes=64)
        for h in range(2):
            cols = slice(h * half, (h + 1) * half)
            nc.vector.tensor_copy(
                w2_bf[:, cols, :].rearrange("p (c i) j -> p c j i", i=4),
                w2_raw[:, :, cols].rearrange("p j (c i) -> p c j i", i=4),
            )
        b_acc = []
        for pair in range(2):
            acc = psum.tile([P, 2, S], F32, name="bacc%d" % pair)
            for e in range(2):
                cols = slice((2 * pair + e) * P, (2 * pair + e + 1) * P)
                nc.tensor.matmul_mx(
                    out=acc[:, e, :], lhsT=d_codes[:, cols].bitcast(FP8X4), lhsT_scale=d_plane[:, cols],
                    rhs=xt_codes[:].bitcast(FP8X4), rhs_scale=xt_plane[:], start=True, stop=True,
                )
            b_acc.append(acc)
        w2_codes = sb.tile([P, N], U32, name="w2_codes", tag="d_codes", align_bytes=64)
        w2_plane = sb.tile([P, N], U8, name="w2_plane", align_bytes=64)
        nc.vector.quantize_mx(
            out=w2_codes[:].bitcast(FP8X4), scales=w2_plane[:], in_=w2_bf[:].rearrange("p c j -> p (c j)")
        )

        z_bf = sb.tile([P, S, PACK], BF16, name="z_bf", tag="w2_bf", align_bytes=64)
        for t in range(TILES):
            nc.scalar.activation(ds[t][:].indirect(n1_t[:]), ra[t // 2][:, t % 2, :], COPY)
            nc.vector.tensor_scalar(z_bf[:, :, t], ds[t][:], gn_t[:, t : t + 1], None, MULT)

        b = sb.tile([P, TILES, S], F32, name="b", tag="d_win", align_bytes=64)
        bg = sb.tile([P, TILES, U], F32, name="bg")
        for pair in range(2):
            nc.scalar.activation(b[:, 2 * pair : 2 * pair + 2, :], b_acc[pair][:], COPY, scale=0.0625)
        for t in range(TILES):
            nc.scalar.activation(bg[:, t, :], b[:, t, :].indirect(n4_t[:]), COPY)

        z_codes = sb.tile([P, S], U32, name="z_codes", align_bytes=64)
        z_plane = sb.tile([P, S], U8, name="z_plane", align_bytes=64)
        nc.vector.quantize_mx(
            out=z_codes[:].bitcast(FP8X4), scales=z_plane[:], in_=z_bf[:].rearrange("p c j -> p (c j)")
        )

        a_acc = []
        for t in range(TILES):
            acc = psum.tile([P, S], F32, name="acc%d" % t)
            cols = slice(t * P, (t + 1) * P)
            nc.tensor.matmul_mx(
                out=acc[:], lhsT=w2_codes[:, cols].bitcast(FP8X4), lhsT_scale=w2_plane[:, cols],
                rhs=z_codes[:].bitcast(FP8X4), rhs_scale=z_plane[:], start=True, stop=True,
            )
            a_acc.append(acc)
        res = []
        ra2 = [sb.tile([P, U], F32, name="ra2_%d" % t) for t in range(TILES)]

        def fetch(t):
            ag = sb.tile([P, U], F32, name="ag%d" % t, tag="ag%d" % t)
            nc.scalar.activation(ag[:], res[t][:].indirect(n3_t[:]), COPY)
            nc.vector.scalar_tensor_tensor(ra2[t][:], ag[:], -0.5, bg[:, t, :], MULT, ADD)

        def put(t):
            nc.scalar.activation(res[t][:].indirect(n3_t[:]), ra2[t][:], COPY)
            nc.sync.dma_start(out[t * P : (t + 1) * P, :], res[t][:])

        def empty(t, copy):
            tag = "ag%d" % (t - 2) if t == 2 else "a%d" % t
            res.append(sb.tile([P, S], F32, name="a%d" % t, tag=tag))
            copy(res[t][:], a_acc[t][:])

        empty(0, nc.vector.tensor_copy)
        empty(1, nc.vector.tensor_copy)
        fetch(0)
        fetch(1)
        empty(2, nc.vector.tensor_copy)
        empty(3, nc.vector.tensor_copy)
        put(0)
        fetch(2)
        fetch(3)
        for t in range(1, TILES):
            put(t)
